import numpy as np
import ml_dtypes


def mxq(x, axis, fmt="e4m3"):
    dtype, down = {"e4m3": (ml_dtypes.float8_e4m3fn, 7), "e5m2": (ml_dtypes.float8_e5m2, 14)}[fmt]
    v = np.moveaxis(np.asarray(x, np.float32).astype(ml_dtypes.bfloat16).astype(np.float64), axis, -1)
    blocks = v.reshape(v.shape[:-1] + (-1, 32))
    amax = np.abs(blocks).max(-1, keepdims=True)
    byte = np.maximum(np.where(amax > 0, np.frexp(amax)[1] - 1 + 127, 0) - down, 1)
    scale = np.exp2(byte - 127.0)
    codes = (blocks / scale).astype(np.float32).astype(dtype).astype(np.float64)
    return np.moveaxis((codes * scale).reshape(v.shape), -1, axis)


WIDE = False


def mx_kscale(k):
    if not WIDE:
        return np.ones(k)
    levels = np.array([10, -10, 5, -5, 0])
    if k % 512:
        return np.exp2(np.random.permutation(np.resize(levels, k // 32))).repeat(32)
    a = np.empty((k // 512, 16))
    for p in range(k // 512):
        a[p, :8] = np.random.permutation(np.resize(levels, 8))
        for g in range(8):
            far = levels[np.abs(levels - a[p, g]) >= 10]
            a[p, g + 8] = far[np.random.randint(len(far))]
    return np.exp2(a.ravel()).repeat(32)


def f64(x):
    return np.asarray(x).astype(np.float64)


def striped8(idx):
    return np.asarray(idx).reshape(8, -1, 16).transpose(0, 2, 1).reshape(128, -1).astype(np.uint16)


def unstriped8(offs):
    return offs.reshape(8, 16, -1).transpose(0, 2, 1).reshape(8, -1).astype(np.int64)


def pick8(x, idx, run):
    r = np.arange(len(x))
    return x[r[:, None], idx[r % (8 * run) // run]]


E2M1 = np.array([0.0, 0.5, 1.0, 1.5, 2.0, 3.0, 4.0, 6.0, -0.0, -0.5, -1.0, -1.5, -2.0, -3.0, -4.0, -6.0])


def pack_weight(w, fmt):
    k, n = w.shape
    w = f64(np.asarray(w, np.float32).astype(ml_dtypes.bfloat16)).reshape(k // 32, 32, n)
    amax = np.abs(w).max(1)
    if fmt == "e4m3":
        byte = np.frexp(amax)[1] - 1 + 127 - 7
    else:
        mant, ex = np.frexp(amax / 6.0)
        byte = np.where(mant > 0.5, ex, ex - 1) + 127
    byte = np.clip(np.where(amax > 0, byte, 1), 1, 254)
    scaled = (w * np.exp2(127.0 - byte)[:, None, :]).reshape(k, n).astype(np.float32)
    by_word = np.ascontiguousarray(scaled.reshape(k // 512, 128, 4, n).transpose(0, 1, 3, 2))
    if fmt == "e4m3":
        words = by_word.astype(ml_dtypes.float8_e4m3fn).view(np.uint8)
    else:
        c = by_word.astype(ml_dtypes.float4_e2m1fn).view(np.uint8) & 0xF
        words = (c[..., 0::2] | (c[..., 1::2] << 4)).reshape(k // 512, 128, 2 * n)
    return np.ascontiguousarray(words), np.ascontiguousarray(byte.astype(np.uint8).reshape(k // 512, 16, n))


def unpack_weight(words, scales, fmt):
    g, _, n = scales.shape
    words = np.ascontiguousarray(words).reshape(g, 128, n, -1)
    if fmt == "e4m3":
        vals = words.view(ml_dtypes.float8_e4m3fn).astype(np.float64)
    else:
        nib = np.empty((g, 128, n, 4), np.uint8)
        nib[..., 0::2] = words & 0xF
        nib[..., 1::2] = words >> 4
        vals = E2M1[nib]
    vals = vals * np.repeat(np.exp2(scales.astype(np.float64) - 127.0), 8, axis=1)[..., None]
    return vals.transpose(0, 1, 3, 2).reshape(g * 512, n)


def sigmoid(v):
    return 1.0 / (1.0 + np.exp(-v))


D, T, I, Q = 512, 1024, 512, 128


def setup_inputs():
    n = np.random.standard_normal
    idx = np.stack([np.random.permutation(T)[:I] for _ in range(8)])
    idx2 = np.stack([np.random.permutation(T)[:I] for _ in range(8)])
    idx3 = np.stack([np.random.permutation(T)[:I] for _ in range(8)])
    idx4 = np.stack([np.random.permutation(T)[:I] for _ in range(8)])
    fd = mx_kscale(D)
    keysp = pack_weight(n((D, T)) / fd[:, None], "e2m1")
    return {
        "query": (n((D, Q)) * 0.9 / np.sqrt(D) * fd[:, None]).astype(np.float32),
        "keys_words": keysp[0],
        "keys_scales": keysp[1],
        "lam": (np.random.uniform(0.3, 0.9, (Q, 1))).astype(np.float32),
        "old": (np.random.uniform(0.3, 1.7, (Q, T))).astype(np.float32),
        "base": (0.5 * n((Q, T))).astype(np.float32),
        "offs": striped8(idx),
        "offs2": striped8(idx2),
        "offs3": striped8(idx3),
        "offs4": striped8(idx4),
    }


def reference(query, keys_words, keys_scales, lam, old, base, offs, offs2, offs3, offs4):
    idx = unstriped8(offs)
    idx2 = unstriped8(offs2)
    idx3 = unstriped8(offs3)
    idx4 = unstriped8(offs4)
    keysu = unpack_weight(keys_words, keys_scales, "e2m1")
    queryq = mxq(f64(query), 0, "e4m3")
    a = queryq.T @ keysu
    s = pick8(a, idx, 16) + np.maximum(pick8(a, idx2, 16), pick8(a, idx3, 16)) * f64(lam)
    w = sigmoid(s)
    ws = w * pick8(f64(old), idx4, 16)
    f1 = np.zeros((Q, T))
    f1[np.arange(Q)[:, None], idx[np.arange(Q) % 128 // 16]] = ws
    y = f64(base) + f1
    return y

from contextlib import ExitStack

import concourse.mybir as mybir

D, T, I, Q = 512, 1024, 512, 128
FLOPS = 2 * D * Q * T

F32 = mybir.dt.float32
BF16 = mybir.dt.bfloat16
I32 = mybir.dt.int32
U32 = mybir.dt.uint32
U16 = mybir.dt.uint16
U8 = mybir.dt.uint8
FP8X4 = mybir.dt.float8_e4m3fn_x4
FP4X4 = mybir.dt.float4_e2m1fn_x4
ALU = mybir.AluOpType
ACT = mybir.ActivationFunctionType

P = 128
PACK = 4
N = 256
HALF = I // 2


def tile_attend_lookahead_lean_timesold_heads_kernel(tc, query, keys_words, keys_scales, lam, old, base, offs, offs2, offs3, offs4, out):
    nc = tc.nc
    with ExitStack() as ctx:
        keep = ctx.enter_context(tc.tile_pool(name="keep", bufs=1))
        psum = ctx.enter_context(tc.psum_pool(name="psum", bufs=1))

        k_scales = keep.tile([P, T], U8, align_bytes=64)
        nc.vector.memset(k_scales[:].bitcast(I32), 0)

        q_raw = keep.tile([P, PACK * Q], F32, tag="staged", name="q_raw")
        nc.sync.dma_start(out=q_raw[:], in_=query.rearrange("(p j) q -> p (j q)", j=PACK))
        for quad in range(4):
            nc.sync.dma_start(
                out=k_scales[32 * quad : 32 * quad + 4, :].bitcast(I32),
                in_=keys_scales[0, 4 * quad : 4 * quad + 4, :].bitcast(I32),
            )
        k_words = keep.tile([P, 2 * T], U8, align_bytes=64)
        nc.sync.dma_start(out=k_words[:].bitcast(I32), in_=keys_words[0].bitcast(I32))
        old_sb = keep.tile([P, T], F32)
        nc.gpsimd.dma_start(out=old_sb[:], in_=old)
        list4 = keep.tile([P, I // 16], U16)
        nc.sync.dma_start(list4[:], offs4)
        list2 = keep.tile([P, I // 16], U16)
        nc.sync.dma_start(list2[:], offs2)
        list3 = keep.tile([P, I // 16], U16)
        nc.sync.dma_start(list3[:], offs3)
        list1 = keep.tile([P, I // 16], U16)
        nc.sync.dma_start(list1[:], offs)

        placed = keep.tile([P, T], F32)
        nc.vector.memset(placed[:], 0.0)

        warm_in = keep.tile([P, 1], F32)
        nc.vector.memset(warm_in[:], 0.0)
        warm_out = keep.tile([P, 1], F32)
        nc.scalar.activation(warm_out[:], warm_in[:], ACT.Sigmoid)

        q_bf = keep.tile([P, Q, PACK], BF16, align_bytes=64, tag="rounded", name="q_bf")
        q_codes = keep.tile([P, Q], U32, align_bytes=64)
        q_scales = keep.tile([P, Q], U8, align_bytes=64)
        q_halves = [slice(0, Q // 2), slice(Q // 2, Q)]
        q_rows = q_raw[:].rearrange("p (t q) -> p t q", t=PACK)
        for rows in q_halves:
            nc.vector.tensor_copy(
                out=q_bf[:, rows, :].rearrange("p (c i) t -> p c t i", i=4),
                in_=q_rows[:, :, rows].rearrange("p t (c i) -> p c t i", i=4),
            )
        for rows in q_halves:
            nc.vector.quantize_mx(
                out=q_codes[:, rows].bitcast(FP8X4),
                scales=q_scales[:, rows],
                in_=q_bf[:, rows, :].rearrange("p q t -> p (q t)"),
            )

        base_sb = keep.tile([P, T], F32, tag="staged", name="base_sb")
        nc.sync.dma_start(out=base_sb[:], in_=base)
        lam_sb = keep.tile([P, 1], F32, align_bytes=64, tag="rounded", name="lam_sb")
        nc.sync.dma_start(out=lam_sb[:], in_=lam)

        halves = [slice(h * HALF // 16, (h + 1) * HALF // 16) for h in range(I // HALF)]
        old_picked = [keep.tile([P, HALF], F32, name="old_picked0")]
        nc.scalar.activation(old_picked[0][:], old_sb[:].indirect(list4[:, halves[0]]), ACT.Copy)

        a = keep.tile([P, T], F32)
        for b in range(T // N):
            bank = psum.tile([P, N], F32, name=f"bank{b}")
            nc.tensor.matmul_mx(
                out=bank[:],
                lhsT=q_codes[:].bitcast(FP8X4),
                lhsT_scale=q_scales[:],
                rhs=k_words[:, 2 * N * b : 2 * N * (b + 1)].bitcast(FP4X4),
                rhs_scale=k_scales[:, N * b : N * (b + 1)],
                start=True,
                stop=True,
            )
            if b % 2 == 0:
                nc.scalar.copy(out=a[:, N * b : N * (b + 1)], in_=bank[:])
            else:
                nc.vector.tensor_copy(out=a[:, N * b : N * (b + 1)], in_=bank[:])

        weights = []
        for h, cols in enumerate(halves):
            first = keep.tile([P, HALF], F32, name=f"first{h}")
            nc.vector.tensor_copy(out=first[:], in_=a[:].indirect(list2[:, cols]))
            second = keep.tile([P, HALF], F32, name=f"second{h}")
            nc.scalar.activation(second[:], a[:].indirect(list3[:, cols]), ACT.Copy)
            own = keep.tile([P, HALF], F32, name=f"own{h}")
            nc.scalar.activation(own[:], a[:].indirect(list1[:, cols]), ACT.Copy)
            larger = keep.tile([P, HALF], F32, name=f"larger{h}")
            nc.vector.tensor_tensor(larger[:], first[:], second[:], ALU.max)
            score = keep.tile([P, HALF], F32, name=f"score{h}")
            nc.vector.scalar_tensor_tensor(score[:], larger[:], lam_sb[:], own[:], ALU.mult, ALU.add)
            weight = keep.tile([P, HALF], F32, name=f"weight{h}")
            nc.scalar.activation(weight[:], score[:], ACT.Sigmoid)
            weights.append(weight)

        clock = keep.tile([P, 1], F32)
        nc.gpsimd.tensor_copy(out=clock[:], in_=weights[0][:, 0:1])
        old_picked.append(keep.tile([P, HALF], F32, tag="score0", name="old_picked1"))
        nc.scalar.activation(old_picked[1][:], old_sb[:].indirect(list4[:, halves[1]]), ACT.Copy)

        for h, cols in enumerate(halves):
            nc.vector.tensor_tensor(placed[:].indirect(list1[:, cols]), weights[h][:], old_picked[h][:], ALU.mult)

        for c in range(T // N):
            cols = slice(N * c, N * (c + 1))
            result = keep.tile([P, N], F32, name=f"result{c}")
            nc.vector.tensor_tensor(result[:], placed[:, cols], base_sb[:, cols], ALU.add)
            queue = nc.sync if c % 2 == 0 else nc.scalar
            queue.dma_start(out=out[:, cols], in_=result[:])
